import numpy as np
import ml_dtypes


def mxq(x, axis, fmt="e4m3"):
    dtype, down = {"e4m3": (ml_dtypes.float8_e4m3fn, 7), "e5m2": (ml_dtypes.float8_e5m2, 14)}[fmt]
    v = np.moveaxis(np.asarray(x, np.float32).astype(ml_dtypes.bfloat16).astype(np.float64), axis, -1)
    blocks = v.reshape(v.shape[:-1] + (-1, 32))
    amax = np.abs(blocks).max(-1, keepdims=True)
    byte = np.maximum(np.where(amax > 0, np.frexp(amax)[1] - 1 + 127, 0) - down, 1)
    scale = np.exp2(byte - 127.0)
    codes = (blocks / scale).astype(np.float32).astype(dtype).astype(np.float64)
    return np.moveaxis((codes * scale).reshape(v.shape), -1, axis)


WIDE = False


def mx_kscale(k):
    if not WIDE:
        return np.ones(k)
    levels = np.array([10, -10, 5, -5, 0])
    if k % 512:
        return np.exp2(np.random.permutation(np.resize(levels, k // 32))).repeat(32)
    a = np.empty((k // 512, 16))
    for p in range(k // 512):
        a[p, :8] = np.random.permutation(np.resize(levels, 8))
        for g in range(8):
            far = levels[np.abs(levels - a[p, g]) >= 10]
            a[p, g + 8] = far[np.random.randint(len(far))]
    return np.exp2(a.ravel()).repeat(32)


def f64(x):
    return np.asarray(x).astype(np.float64)


def striped8(idx):
    return np.asarray(idx).reshape(8, -1, 16).transpose(0, 2, 1).reshape(128, -1).astype(np.uint16)


def unstriped8(offs):
    return offs.reshape(8, 16, -1).transpose(0, 2, 1).reshape(8, -1).astype(np.int64)


def pick8(x, idx, run):
    r = np.arange(len(x))
    return x[r[:, None], idx[r % (8 * run) // run]]


E2M1 = np.array([0.0, 0.5, 1.0, 1.5, 2.0, 3.0, 4.0, 6.0, -0.0, -0.5, -1.0, -1.5, -2.0, -3.0, -4.0, -6.0])


def pack_weight(w, fmt):
    k, n = w.shape
    w = f64(np.asarray(w, np.float32).astype(ml_dtypes.bfloat16)).reshape(k // 32, 32, n)
    amax = np.abs(w).max(1)
    if fmt == "e4m3":
        byte = np.frexp(amax)[1] - 1 + 127 - 7
    else:
        mant, ex = np.frexp(amax / 6.0)
        byte = np.where(mant > 0.5, ex, ex - 1) + 127
    byte = np.clip(np.where(amax > 0, byte, 1), 1, 254)
    scaled = (w * np.exp2(127.0 - byte)[:, None, :]).reshape(k, n).astype(np.float32)
    by_word = np.ascontiguousarray(scaled.reshape(k // 512, 128, 4, n).transpose(0, 1, 3, 2))
    if fmt == "e4m3":
        words = by_word.astype(ml_dtypes.float8_e4m3fn).view(np.uint8)
    else:
        c = by_word.astype(ml_dtypes.float4_e2m1fn).view(np.uint8) & 0xF
        words = (c[..., 0::2] | (c[..., 1::2] << 4)).reshape(k // 512, 128, 2 * n)
    return np.ascontiguousarray(words), np.ascontiguousarray(byte.astype(np.uint8).reshape(k // 512, 16, n))


def unpack_weight(words, scales, fmt):
    g, _, n = scales.shape
    words = np.ascontiguousarray(words).reshape(g, 128, n, -1)
    if fmt == "e4m3":
        vals = words.view(ml_dtypes.float8_e4m3fn).astype(np.float64)
    else:
        nib = np.empty((g, 128, n, 4), np.uint8)
        nib[..., 0::2] = words & 0xF
        nib[..., 1::2] = words >> 4
        vals = E2M1[nib]
    vals = vals * np.repeat(np.exp2(scales.astype(np.float64) - 127.0), 8, axis=1)[..., None]
    return vals.transpose(0, 1, 3, 2).reshape(g * 512, n)


def sigmoid(v):
    return 1.0 / (1.0 + np.exp(-v))


D, T, I, Q = 512, 1024, 512, 128


def setup_inputs():
    n = np.random.standard_normal
    idx = np.stack([np.random.permutation(T)[:I] for _ in range(8)])
    idx2 = np.stack([np.random.permutation(T)[:I] for _ in range(8)])
    idx3 = np.stack([np.random.permutation(T)[:I] for _ in range(8)])
    idx4 = np.stack([np.random.permutation(T)[:I] for _ in range(8)])
    fd = mx_kscale(D)
    keysp = pack_weight(n((D, T)) / fd[:, None], "e2m1")
    return {
        "query": (n((D, Q)) * 1.2 / np.sqrt(D) * fd[:, None]).astype(np.float32),
        "keys_words": keysp[0],
        "keys_scales": keysp[1],
        "lam": (np.random.uniform(0.5, 1.5, (Q, 1))).astype(np.float32),
        "old": (1.0 * n((Q, T))).astype(np.float32),
        "offs": striped8(idx),
        "offs2": striped8(idx2),
        "offs3": striped8(idx3),
        "offs4": striped8(idx4),
    }


def reference(query, keys_words, keys_scales, lam, old, offs, offs2, offs3, offs4):
    idx = unstriped8(offs)
    idx2 = unstriped8(offs2)
    idx3 = unstriped8(offs3)
    idx4 = unstriped8(offs4)
    keysu = unpack_weight(keys_words, keys_scales, "e2m1")
    queryq = mxq(f64(query), 0, "e4m3")
    a = queryq.T @ keysu
    g1 = sigmoid(pick8(a, idx2, 16) * 2.0)
    w = (pick8(a, idx, 16) * g1 + pick8(a, idx3, 16) * (1.0 - g1)) * f64(lam)
    f1 = np.zeros((Q, T))
    f1[np.arange(Q)[:, None], idx4[np.arange(Q) % 128 // 16]] = w
    y = f64(old) + f1
    return y

from contextlib import ExitStack

import concourse.mybir as mybir

D, T, SLOTS, Q = 512, 1024, 512, 128
FLOPS = 2 * D * T * Q

F32 = mybir.dt.float32
BF16 = mybir.dt.bfloat16
I32 = mybir.dt.int32
U32 = mybir.dt.uint32
U16 = mybir.dt.uint16
U8 = mybir.dt.uint8
FP8X4 = mybir.dt.float8_e4m3fn_x4
FP4X4 = mybir.dt.float4_e2m1fn_x4
ALU = mybir.AluOpType
ACT = mybir.ActivationFunctionType

P = 128
PACK = 4
N_TILE = 256
HALF = SLOTS // 2
STORE_COLS = 256


def tile_attend_conditioned_lean_putold_heads_kernel(
    tc, query, keys_words, keys_scales, lam, old, offs, offs2, offs3, offs4, out
):
    nc = tc.nc
    with ExitStack() as ctx:
        lists = ctx.enter_context(tc.tile_pool(name="lists", bufs=1))
        sb = ctx.enter_context(tc.tile_pool(name="sb", bufs=1))
        psum = ctx.enter_context(tc.psum_pool(name="psum", bufs=1))

        k_scales = sb.tile([P, T], U8, align_bytes=64)
        nc.vector.memset(k_scales[:].bitcast(I32), 0)

        q_raw = sb.tile([P, PACK, Q], F32)
        nc.sync.dma_start(out=q_raw[:], in_=query.rearrange("(p j) q -> p j q", j=PACK))
        k_words = sb.tile([P, 2 * T], U8, align_bytes=64)
        nc.sync.dma_start(out=k_words[:].bitcast(I32), in_=keys_words[0].bitcast(I32))
        for quad in range(4):
            nc.sync.dma_start(
                out=k_scales[32 * quad : 32 * quad + 4, :].bitcast(I32),
                in_=keys_scales[0, 4 * quad : 4 * quad + 4, :].bitcast(I32),
            )
        judge_offs = lists.tile([P, SLOTS // 16], U16)
        nc.sync.dma_start(judge_offs[:], offs2)
        first_offs = lists.tile([P, SLOTS // 16], U16)
        nc.sync.dma_start(first_offs[:], offs)
        lam_col = sb.tile([P, 1], F32)
        nc.sync.dma_start(out=lam_col[:], in_=lam)
        place_offs = lists.tile([P, SLOTS // 16], U16)
        nc.sync.dma_start(place_offs[:], offs4)
        second_offs = lists.tile([P, SLOTS // 16], U16)
        nc.sync.dma_start(second_offs[:], offs3)
        old_sb = sb.tile([P, T], F32)
        nc.sync.dma_start(out=old_sb[:], in_=old)

        placed = sb.tile([P, T], F32)
        nc.vector.memset(placed[:], 0.0)

        q_bf = sb.tile([P, Q, PACK], BF16, align_bytes=64)
        nc.vector.tensor_copy(
            out=q_bf[:].rearrange("p (c i) t -> p c t i", i=4),
            in_=q_raw[:].rearrange("p t (c i) -> p c t i", i=4),
        )
        q_codes = sb.tile([P, Q], U32, align_bytes=64)
        q_scales = sb.tile([P, Q], U8, align_bytes=64)
        nc.vector.quantize_mx(
            out=q_codes[:].bitcast(FP8X4),
            scales=q_scales[:],
            in_=q_bf[:].rearrange("p q t -> p (q t)"),
        )

        neg_lam = sb.tile([P, HALF], F32)
        nc.gpsimd.tensor_scalar(neg_lam[:], lam_col[:].to_broadcast([P, HALF]), -1.0, 0.0, ALU.mult, ALU.add)

        a = sb.tile([P, T], F32)
        for n0 in range(0, T, N_TILE):
            acc = psum.tile([P, N_TILE], F32, name="acc%d" % n0)
            nc.tensor.matmul_mx(
                out=acc[:],
                lhsT=q_codes[:].bitcast(FP8X4),
                lhsT_scale=q_scales[:],
                rhs=k_words[:, 2 * n0 : 2 * (n0 + N_TILE)].bitcast(FP4X4),
                rhs_scale=k_scales[:, n0 : n0 + N_TILE],
                start=True,
                stop=True,
            )
            nc.vector.tensor_copy(out=a[:, n0 : n0 + N_TILE], in_=acc[:])

        gate = sb.tile([P, SLOTS], F32)
        first = sb.tile([P, SLOTS], F32)
        second = sb.tile([P, HALF], F32)
        neg_second = sb.tile([P, HALF], F32)
        u = sb.tile([P, SLOTS], F32)
        v = sb.tile([P, SLOTS], F32)
        lo, hi = slice(0, HALF), slice(HALF, SLOTS)
        lo16, hi16 = slice(0, HALF // 16), slice(HALF // 16, SLOTS // 16)

        nc.scalar.activation(gate[:, lo], a[:].indirect(judge_offs[:, lo16]), ACT.Sigmoid, scale=2.0)
        nc.vector.tensor_copy(first[:, lo], a[:].indirect(first_offs[:, lo16]))
        nc.vector.tensor_tensor(neg_second[:], a[:].indirect(second_offs[:, lo16]), neg_lam[:], ALU.mult)
        nc.scalar.activation(gate[:, hi], a[:].indirect(judge_offs[:, hi16]), ACT.Sigmoid, scale=2.0)
        nc.scalar.activation(first[:, hi], a[:].indirect(first_offs[:, hi16]), ACT.Copy)
        nc.scalar.activation(second[:], a[:].indirect(second_offs[:, hi16]), ACT.Copy)

        def first_term(s):
            nc.vector.scalar_tensor_tensor(u[:, s], first[:, s], lam_col[:], gate[:, s], ALU.mult, ALU.mult)

        def second_term(s):
            nc.vector.scalar_tensor_tensor(v[:, s], gate[:, s], 1.0, neg_second[:], ALU.subtract, ALU.mult)

        def place(s, s16):
            nc.vector.tensor_tensor(placed[:].indirect(place_offs[:, s16]), u[:, s], v[:, s], ALU.add)

        first_term(lo)
        second_term(lo)
        nc.scalar.activation(neg_second[:], second[:], ACT.Copy, scale=neg_lam[:, 0:1])
        first_term(hi)
        place(lo, lo16)
        second_term(hi)
        place(hi, hi16)

        total = sb.tile([P, T], F32)
        for n0 in range(0, T, STORE_COLS):
            c = slice(n0, n0 + STORE_COLS)
            nc.vector.tensor_tensor(total[:, c], old_sb[:, c], placed[:, c], ALU.add)
            nc.sync.dma_start(out=out[:, c], in_=total[:, c])
